import numpy as np, ml_dtypes
CORES = [48,51,52,55]
N = 4
import mx_ref
BF = ml_dtypes.bfloat16
def entries(a):
    return np.ascontiguousarray(a.T).reshape(-1)
def table(e):
    return np.ascontiguousarray(np.reshape(e, (-1, 16)).T).astype(np.int32)
def cols(t, e):
    v = np.concatenate([t.reshape(128, -1, 4), np.zeros((128, 1, 4), BF)], axis=1)
    return np.ascontiguousarray(v[:, e]).reshape(128, -1)
def pick(q, e):
    c = np.concatenate([q[0].reshape(128, -1, 4), np.zeros((128, 1, 4), np.uint8)], axis=1); s = np.concatenate([q[1], np.ones((16, 1), np.uint8)], axis=1)
    return (np.ascontiguousarray(c[:, e].reshape(128, -1)), np.ascontiguousarray(s[:, e]))
def join(*qs):
    return (np.concatenate([q[0] for q in qs], axis=1), np.concatenate([q[1] for q in qs], axis=1))
def put(q, e, v):
    c, s = q[0].reshape(128, -1, 4).copy(), q[1].copy(); c[:, e] = v[0].reshape(128, -1, 4); s[:, e] = v[1]
    return (c.reshape(128, -1), s)
def pk(c, s):
    return (np.ascontiguousarray(c), mx_ref.live(s))
def emit(q):
    return q[0], q[1]
def decode(q):
    o = []
    for b in range(4):
        e = np.zeros((128, 128, 4), np.float32); e[np.arange(128), np.arange(128), b] = 1
        o.append(mx_ref.matmul(mx_ref.quantize(e.reshape(128, 512).astype(BF)), q))
    return np.stack(o, axis=2).reshape(128, -1)
def f(rng, *shape):
    return mx_ref.flush((rng.standard_normal(shape, dtype=np.float32) * np.exp2(rng.integers(-2, 3, shape[:-1] + (1,)))).astype(BF))
def wide(rng, *shape, cols=0):
    v = rng.standard_normal(shape, dtype=np.float32) * np.exp2(rng.integers(-12, 13, shape)).astype(np.float32)
    if cols: v *= np.repeat(np.exp2(rng.integers(-cols, cols + 1, shape[:-2] + (1, shape[-1] // 4))) * (rng.random(shape[:-2] + (1, shape[-1] // 4)) > 0.0625), 4, axis=-1).astype(np.float32)
    return mx_ref.flush(v.astype(BF))
T, CAPP = 512, 128
def lists(rng, count, high=False, among=T, unnamed=0):
    sn, so = np.full((N, N * CAPP), -1), np.zeros((N, 512), int)
    for d in range(N):
        filled = []
        for s in range(N):
            c = np.sort(rng.permutation(CAPP)[:count[s, d]]); k = rng.permutation(among)[:c.size]
            sn[s, d * CAPP + c] = np.sort(k)[::-1] if high else k
            filled.append(s * CAPP + c)
        filled = np.concatenate(filled)
        if unnamed: filled = rng.permutation(filled)[unnamed:]
        o = np.concatenate([filled, rng.choice(filled, 512 - filled.size)])
        so[d] = np.sort(o)[::-1] if high else rng.permutation(o)
    return {"sn": np.stack([table(v) for v in sn]), "so": np.stack([table(v) for v in so])}
def setup_inputs(rng):
    return {"x": f(rng, N, 128, 4 * T), **lists(rng, rng.integers(1, CAPP + 1, (N, N)))}
def setup_inputs_full(rng):
    return {**setup_inputs(rng), **lists(rng, np.full((N, N), CAPP))}
def setup_inputs_one(rng):
    n = np.zeros((N, N), int); n[rng.integers(0, N)] = 3
    return {**setup_inputs(rng), **lists(rng, n, among=rng.permutation(T)[:3])}
def setup_inputs_own(rng):
    return {**setup_inputs(rng), **lists(rng, CAPP * np.eye(N, dtype=int))}
def setup_inputs_reversed(rng):
    return {**setup_inputs(rng), **lists(rng, rng.integers(1, CAPP + 1, (N, N)), high=True, unnamed=3)}
def setup_inputs_spread(rng):
    d = setup_inputs(rng); d["x"] = wide(rng, N, 128, 4 * T, cols=8); return d
def check_inputs(d):
    b = []
    a = np.stack([entries(d["sn"][s]) for s in range(N)])
    for r in range(N):
        pairs = [a[r, q * CAPP:q * CAPP + CAPP] for q in range(N)]
        if a[r].min() < -1 or a[r].max() >= T or any(len(set(g[g >= 0].tolist())) != (g >= 0).sum() for g in pairs): b.append("sn")
        e = entries(d["so"][r])
        if e.min() < 0 or e.max() >= N * CAPP: b.append("so")
        elif (a[e // CAPP, r * CAPP + e % CAPP] < 0).any(): b.append("so")
    return b
def reference(x, sn, so):
    v = np.concatenate([x[s] for s in range(N)], axis=1)
    a = np.stack([entries(sn[s]) for s in range(N)])
    fc, fs = np.zeros((N, 128, 2048), np.uint8), np.zeros((N, 16, 512), np.uint8)
    bc, bs = np.zeros((N, 128, 2048), np.uint8), np.zeros((N, 16, 512), np.uint8)
    for d in range(N):
        e = entries(so[d]); s = e // CAPP
        F = mx_ref.quantize(cols(v, s * T + a[s, d * CAPP + e % CAPP]))
        fc[d], fs[d] = emit(F)
        m = decode(F).reshape(128, 512, 4).transpose(0, 2, 1).reshape(512, 512)
        m = np.ascontiguousarray(m.T).astype(BF)
        bt = []
        for b in range(4):
            k = np.ascontiguousarray(m[:, 128 * b:128 * b + 128]).reshape(128, 4, 128)
            bt.append(mx_ref.quantize(np.ascontiguousarray(k.transpose(0, 2, 1)).reshape(128, 512)))
        bc[d], bs[d] = emit(join(*bt))
    return {"fc": fc, "fs": fs, "bc": bc, "bs": bs}

@@ -1,0 +1,226 @@
+from concourse.bass import DstId, RemoteDMATransfer
+from concourse.mybir import dt, AluOpType, ActivationFunctionType
+
+N = 4
+CAPP = 128
+TOK = 512
+XA = 336
+PART = 32
+ZV = 480
+RUNS = ((0, 256), (256, 512))
+COPY_V = (2, 3)
+COPY_S = (0, 1)
+
+SCRATCH = {
+    "xt": ("sbuf", [128, 4 * TOK], "bfloat16"),
+    "sn2": ("sbuf", [32, 32], "int32"),
+    "lst": ("sbuf", [128, 32], "uint16"),
+    "m2": ("sbuf", [32, 4, 32], "int32"),
+    "lp": ("sbuf", [128, 32], "uint16"),
+    "s2": ("sbuf", [64, 32], "int32"),
+    "ln": ("sbuf", [128, 32], "uint16"),
+    "ones": ("sbuf", [128, 128], "bfloat16"),
+    "ident": ("sbuf", [128, 128], "bfloat16"),
+    "et": ("sbuf", [128, 2048], "bfloat16"),
+    "pp": ("psum", [128, 2048], "float32"),
+    "bt": ("sbuf", [128, 2048], "bfloat16"),
+}
+for _n, _w in (("x", 512), ("slot", 512), ("land", 512), ("e", 512), ("fp", 512), ("fn", 512), ("bt", 512)):
+    SCRATCH[_n + "q"] = ("sbuf", [128, _w], "float8_e4m3fn_x4")
+    SCRATCH[_n + "s"] = ("sbuf", [128, _w], "uint8")
+SEMAPHORES = (
+    ["x0", "x1", "snl", "m2l", "s2l", "stsy", "stsc", "vones", "vez", "vea", "vezb", "sez", "gida", "gidb", "veb",
+     "veqa", "veqb", "arre", "qx", "vlst", "ownc", "owns",
+     "vln", "vlp", "snd", "arrc", "arrs", "fnc", "fnsc", "q0", "q1", "cv", "cs"]
+    + ["pc%d" % i for i in range(3)] + ["ps%d" % i for i in range(3)]
+    + ["fc%d" % h for h in range(2)] + ["fs%d" % h for h in range(2)]
+    + ["mm%d" % t for t in range(4)])
+
+
+def receivers(src, cores, topo):
+    mine = [c for c in cores if topo.die(c) == topo.die(src)]
+    far = [c for c in cores if topo.die(c) != topo.die(src)]
+    k = mine.index(src)
+    far = far[k:] + far[:k]
+    near = [c for c in mine if c != src]
+    out = []
+    for i, c in enumerate(far[:1] + near + far[1:]):
+        e = topo.engines(src, c)
+        a, b = e[0::2], e[1::2]
+        h = len(b) // 2
+        out.append((c, (a, b, a)[i], (b[:h], a, b[h:])[i]))
+    return out
+
+
+def bits(engines):
+    m = 0
+    for e in engines:
+        m |= 1 << e
+    return m
+
+
+def rank_program(g, core, T, topo):
+    rank = T.rank_of(core)
+    if rank is None:
+        return
+    S = T.sem
+    v, sc, te, sy = g.vector, g.scalar, g.tensor, g.sync
+    Copy = ActivationFunctionType.Copy
+    u32, u8 = dt.uint32, dt.uint8
+
+    for k, q in enumerate((sy, sc)):
+        q.dma_start(T.sn2[16 * k:16 * k + 16, :], T.sn[:]).then_inc(S.snl, 16)
+    sy.dma_start(T.xt[:, 0:4 * XA], T.x[:, 0:4 * XA]).then_inc(S.x0, 16)
+    sy.dma_start(T.xt[:, 4 * XA:4 * TOK], T.x[:, 4 * XA:4 * TOK]).then_inc(S.x1, 16)
+    for k in range(2):
+        for q in range(4):
+            r = 16 * k + 4 * q
+            sy.dma_start(T.m2[r:r + 4, :, 0:32 - q], T.so[:, q:32]).then_inc(S.m2l, 16)
+    for k in range(4):
+        sy.dma_start(T.s2[16 * k:16 * k + 16, :], T.so[:]).then_inc(S.s2l, 16)
+
+    plan = receivers(core, T.cores, topo)
+    pal = [dst for dst, _, _ in plan if topo.die(dst) == topo.die(core)][0]
+    low = rank < T.rank_of(pal)
+    first = (0, 128) if low else (TOK - 128, TOK)
+    give = (0, PART) if low else (TOK - PART, TOK)
+    rest = (128, TOK - PART) if low else (PART, TOK - 128)
+    z0, z1 = 4 * rest[0], 4 * rest[1]
+    v.memset(T.ones[:], 1.0).then_inc(S.vones, 1)
+    v.memset(T.et[:, 4 * first[0]:4 * first[1]], 0.0).then_inc(S.vez, 1)
+    v.memset(T.et[:, z0:z0 + ZV], 0.0).then_inc(S.vezb, 1)
+    sc.wait_ge(S.vezb, 1)
+    parts = range(z0 + ZV, z1, ZV)
+    for a in parts:
+        w = min(ZV, z1 - a)
+        sc.activation(T.et[:, a:a + w], T.et[:, z0:z0 + w], Copy).then_inc(S.sez, 1)
+    g.wait_ge(S.vones, 1)
+    for (lo, hi), sem in ((first, S.gida), (rest, S.gidb)):
+        a, b = lo // 4, hi // 4
+        g.affine_select(T.ident[:, a:b], T.ones[:, a:b], [[-1, b - a]], AluOpType.is_equal, 0.0, -a, 1).then_inc(sem, 1)
+
+    def ones_of(cols, sem):
+        for t in range(4):
+            v.tensor_copy(T.et[:, 4 * cols[0] + 5 * t:4 * cols[1]:16], T.ident[:, cols[0] // 4:cols[1] // 4]).then_inc(sem, 1)
+
+    v.wait_ge(S.vez, 1)
+    v.wait_ge(S.gida, 1)
+    ones_of(first, S.vea)
+    v.wait_ge(S.vea, 4)
+    v.quantize_mx(T.eq[:, first[0]:first[1]], T.es[:, first[0]:first[1]],
+                  T.et[:, 4 * first[0]:4 * first[1]]).then_inc(S.veqa, 1)
+    rid, pid, _ = topo.addr(pal)
+    every = topo.engines(core, pal)
+    cut = slice(*give)
+    g.wait_ge(S.veqa, 1)
+    for part in (T.eq[:, cut].bitcast(u8), T.es[:, cut]):
+        g.remote_dma_fused([RemoteDMATransfer(dst_ids=[DstId(rid=rid, pnc=pid)], dma_engine_mask=bits(every),
+                                              remote_sem=S.arre, src=part, dst=part)], local_sem=S.snd)
+
+    v.wait_ge(S.snl, 32)
+    for k in range(4):
+        v.tensor_copy(T.lst[32 * k:32 * k + 32, :], T.sn2[:]).then_inc(S.vlst, 1)
+    v.wait_ge(S.x0, 16)
+    v.quantize_mx(T.xq[:, 0:XA], T.xs[:, 0:XA], T.xt[:, 0:4 * XA]).then_inc(S.qx, 1)
+    v.wait_ge(S.x1, 16)
+    v.quantize_mx(T.xq[:, XA:TOK], T.xs[:, XA:TOK], T.xt[:, 4 * XA:4 * TOK]).then_inc(S.qx, 1)
+
+    for q in (v, sc):
+        q.wait_ge(S.vlst, 4)
+        q.wait_ge(S.qx, 2)
+
+    def pick(d, code, scale, c_sem, s_sem):
+        lo, hi = CAPP * d, CAPP * (d + 1)
+        off = T.lst[:, 8 * d:8 * d + 8]
+        v.tensor_copy(code[:, lo:hi].bitcast(u32), T.xq[:, 0:TOK].bitcast(u32).indirect(off)).then_inc(c_sem, 1)
+        sc.activation(scale[:, lo:hi], T.xs[:, 0:TOK].indirect(off), Copy).then_inc(s_sem, 1)
+
+    own = slice(CAPP * rank, CAPP * (rank + 1))
+    codes, scales = [], []
+    for i, (dst, ec, es) in enumerate(plan):
+        d = T.rank_of(dst)
+        pick(d, T.slotq, T.slots, S["pc%d" % i], S["ps%d" % i])
+        rid, pid, _ = topo.addr(dst)
+        cut = slice(CAPP * d, CAPP * (d + 1))
+        codes.append(RemoteDMATransfer(dst_ids=[DstId(rid=rid, pnc=pid)], dma_engine_mask=bits(ec), remote_sem=S.arrc,
+                                       src=T.slotq[:, cut].bitcast(u8), dst=T.landq[:, own].bitcast(u8)))
+        scales.append(RemoteDMATransfer(dst_ids=[DstId(rid=rid, pnc=pid)], dma_engine_mask=bits(es), remote_sem=S.arrs,
+                                        src=T.slots[:, cut], dst=T.lands[:, own]))
+    pick(rank, T.landq, T.lands, S.ownc, S.owns)
+    g.wait_ge(S.pc0, 1)
+    g.remote_dma_fused(codes[:1], local_sem=S.snd)
+    g.wait_ge(S.pc1, 1)
+    g.wait_ge(S.pc2, 1)
+    g.remote_dma_fused(codes[1:], local_sem=S.snd)
+    for i in range(3):
+        g.wait_ge(S["ps%d" % i], 1)
+    g.remote_dma_fused(scales, local_sem=S.snd)
+    g.wait_ge(S.snd, 2 * len(every) + sum(len(ec) + len(es) for _, ec, es in plan))
+    arrive = [e for src in T.cores for e in receivers(src, T.cores, topo) if e[0] == core]
+
+    v.wait_ge(S.gidb, 1)
+    v.wait_ge(S.vezb, 1)
+    v.wait_ge(S.sez, len(parts))
+    ones_of(rest, S.veb)
+    v.wait_ge(S.m2l, 16 * 8)
+    for k in range(4):
+        v.tensor_copy(T.lp[32 * k:32 * k + 32, :], T.m2[:, :, 0:32:4]).then_inc(S.vlp, 1)
+    v.wait_ge(S.veb, 4)
+    v.quantize_mx(T.eq[:, rest[0]:rest[1]], T.es[:, rest[0]:rest[1]], T.et[:, z0:z1]).then_inc(S.veqb, 1)
+    v.wait_ge(S.s2l, 16 * 4)
+    for k in range(2):
+        v.tensor_copy(T.ln[64 * k:64 * k + 64, :], T.s2[:]).then_inc(S.vln, 1)
+
+    te.wait_ge(S.veqa, 1)
+    te.wait_ge(S.veqb, 1)
+    te.wait_ge(S.arre, 2 * len(topo.engines(pal, core)))
+    for t in range(4):
+        te.wait_ge(S["fc%d" % (t // 2)], 1)
+        te.wait_ge(S["fs%d" % (t // 2)], 1)
+        te.matmul_mx(T.pp[:, 512 * t:512 * t + 512], T.fpq[:, 128 * t:128 * t + 128], T.fps[:, 128 * t:128 * t + 128],
+                     T.eq[:, 0:512], T.es[:, 0:512], True, True).then_inc(S["mm%d" % t], 1)
+
+    v.wait_ge(S.vlp, 4)
+    v.wait_ge(S.ownc, 1)
+    v.wait_ge(S.arrc, sum(len(ec) for _, ec, _ in arrive))
+    for h in range(2):
+        v.tensor_copy(T.fpq[:, 256 * h:256 * h + 256].bitcast(u32),
+                      T.landq[:, 0:512].bitcast(u32).indirect(T.lp[:, 16 * h:16 * h + 16])).then_inc(S["fc%d" % h], 1)
+    v.wait_ge(S.vln, 2)
+    v.tensor_copy(T.fnq[:, 0:512].bitcast(u32),
+                  T.landq[:, 0:512].bitcast(u32).indirect(T.ln[:, 0:32])).then_inc(S.fnc, 1)
+    for t in COPY_V:
+        v.wait_ge(S["mm%d" % t], 1)
+        v.tensor_copy(T.bt[:, t:2048:4], T.pp[:, 512 * t:512 * t + 512]).then_inc(S.cv, 1)
+    v.wait_ge(S.cs, len(COPY_S))
+    v.wait_ge(S.cv, len(COPY_V))
+    for h, (lo, hi) in enumerate(RUNS):
+        v.quantize_mx(T.btq[:, lo:hi], T.bts[:, lo:hi], T.bt[:, 4 * lo:4 * hi]).then_inc(S["q%d" % h], 1)
+
+    sc.wait_ge(S.vlp, 4)
+    sc.wait_ge(S.owns, 1)
+    sc.wait_ge(S.arrs, sum(len(es) for _, _, es in arrive))
+    for h in range(2):
+        sc.activation(T.fps[:, 256 * h:256 * h + 256],
+                      T.lands[:, 0:512].indirect(T.lp[:, 16 * h:16 * h + 16]), Copy).then_inc(S["fs%d" % h], 1)
+    for t in COPY_S:
+        sc.wait_ge(S["mm%d" % t], 1)
+        sc.activation(T.bt[:, t:2048:4], T.pp[:, 512 * t:512 * t + 512], Copy).then_inc(S.cs, 1)
+    sc.wait_ge(S.vln, 2)
+    sc.activation(T.fns[:, 0:512], T.lands[:, 0:512].indirect(T.ln[:, 0:32]), Copy).then_inc(S.fnsc, 1)
+
+    sy.wait_ge(S.fnc, 1)
+    sy.dma_start(T.fc[:, 0:2048], T.fnq[:, 0:512].bitcast(u8)).then_inc(S.stsy, 16)
+    for h, (lo, hi) in enumerate(RUNS):
+        sy.wait_ge(S["q%d" % h], 1)
+        sy.dma_start(T.bc[:, 4 * lo:4 * hi], T.btq[:, lo:hi].bitcast(u8)).then_inc(S.stsy, 16)
+    for k in range(3):
+        sy.dma_start(T.bs[4 * k:4 * k + 4, 0:512], T.bts[32 * k:32 * k + 4, 0:512]).then_inc(S.stsy, 16)
+    sc.wait_ge(S.fnsc, 1)
+    for k in range(4):
+        sc.dma_start(T.fs[4 * k:4 * k + 4, 0:512], T.fns[32 * k:32 * k + 4, 0:512]).then_inc(S.stsc, 16)
+    sc.wait_ge(S.q0, 1)
+    sc.wait_ge(S.q1, 1)
+    sc.dma_start(T.bs[12:16, 0:512], T.bts[96:100, 0:512]).then_inc(S.stsc, 16)
+    sy.wait_ge(S.stsy, 16 * 6)
+    sc.wait_ge(S.stsc, 16 * 5)

@@ -4,12 +4,16 @@ from concourse.mybir import dt, AluOpType, ActivationFunctionType
 N = 4
 CAPP = 128
 TOK = 512
-XA = 336
+XCUT = (0, 336, 512)
 PART = 32
 ZV = 480
-RUNS = ((0, 256), (256, 512))
-COPY_V = (2, 3)
-COPY_S = (0, 1)
+ONES = "sl"
+SENDS = (("c0",), ("s0",), ("c1",), ("s1",), ("c2",), ("s2",))
+RECV = "ffn"
+MM = [(t, 0, 512) for t in range(4)]
+VQ = [("pc", 0, 256), ("pc", 256, 512), ("nc", 0, 512), ("cp", 2), ("cp", 3), ("q", 0, 256), ("q", 256, 512)]
+SQ = [("ps", 0, 256), ("ps", 256, 512), ("cp", 0), ("cp", 1), ("ns", 0, 512), ("fs", 0), ("fs", 1), ("fs", 2), ("fs", 3), ("bs", 3)]
+YQ = [("fc", 0, 512), ("bc", 0, 256), ("bc", 256, 512), ("bs", 0), ("bs", 1), ("bs", 2)]
 
 SCRATCH = {
     "xt": ("sbuf", [128, 4 * TOK], "bfloat16"),
@@ -22,19 +26,25 @@ SCRATCH = {
     "ones": ("sbuf", [128, 128], "bfloat16"),
     "ident": ("sbuf", [128, 128], "bfloat16"),
     "et": ("sbuf", [128, 2048], "bfloat16"),
-    "pp": ("psum", [128, 2048], "float32"),
+    "pp": ("psum", [128, 4096], "float32"),
     "bt": ("sbuf", [128, 2048], "bfloat16"),
 }
 for _n, _w in (("x", 512), ("slot", 512), ("land", 512), ("e", 512), ("fp", 512), ("fn", 512), ("bt", 512)):
     SCRATCH[_n + "q"] = ("sbuf", [128, _w], "float8_e4m3fn_x4")
     SCRATCH[_n + "s"] = ("sbuf", [128, _w], "uint8")
+
+
+def name(item):
+    return item[0] + str(item[1])
+
+
 SEMAPHORES = (
-    ["x0", "x1", "snl", "m2l", "s2l", "stsy", "stsc", "vones", "vez", "vea", "vezb", "sez", "gida", "gidb", "veb",
-     "veqa", "veqb", "arre", "qx", "vlst", "ownc", "owns",
-     "vln", "vlp", "snd", "arrc", "arrs", "fnc", "fnsc", "q0", "q1", "cv", "cs"]
-    + ["pc%d" % i for i in range(3)] + ["ps%d" % i for i in range(3)]
-    + ["fc%d" % h for h in range(2)] + ["fs%d" % h for h in range(2)]
-    + ["mm%d" % t for t in range(4)])
+    ["snl", "m2l", "s2l", "stsy", "stsc", "vones", "vez", "vea", "vezb", "sez", "gida", "gidb", "veb",
+     "veqa", "veqb", "arre", "qx", "vlst", "ownc", "owns", "vln", "vlp", "snd", "arrc", "arrs"]
+    + ["x%d" % i for i in range(len(XCUT) - 1)]
+    + ["kc%d" % i for i in range(3)] + ["ks%d" % i for i in range(3)]
+    + ["mm%d" % t for t in range(len(MM))]
+    + [name(i) for i in VQ + SQ if i[0] not in ("fs", "bs", "fc", "bc")])
 
 
 def receivers(src, cores, topo):
@@ -43,13 +53,14 @@ def receivers(src, cores, topo):
     k = mine.index(src)
     far = far[k:] + far[:k]
     near = [c for c in mine if c != src]
-    out = []
-    for i, c in enumerate(far[:1] + near + far[1:]):
-        e = topo.engines(src, c)
-        a, b = e[0::2], e[1::2]
-        h = len(b) // 2
-        out.append((c, (a, b, a)[i], (b[:h], a, b[h:])[i]))
-    return out
+    pool = {"f": far, "n": near}
+    return [pool[w].pop(0) for w in RECV]
+
+
+def sends(src, cores, topo):
+    plan = receivers(src, cores, topo)
+    return [[(w[0], int(w[1]), plan[int(w[1])], topo.engines(src, plan[int(w[1])])[k::len(call)])
+             for k, w in enumerate(call)] for call in SENDS]
 
 
 def bits(engines):
@@ -70,8 +81,9 @@ def rank_program(g, core, T, topo):
 
     for k, q in enumerate((sy, sc)):
         q.dma_start(T.sn2[16 * k:16 * k + 16, :], T.sn[:]).then_inc(S.snl, 16)
-    sy.dma_start(T.xt[:, 0:4 * XA], T.x[:, 0:4 * XA]).then_inc(S.x0, 16)
-    sy.dma_start(T.xt[:, 4 * XA:4 * TOK], T.x[:, 4 * XA:4 * TOK]).then_inc(S.x1, 16)
+    for i in range(len(XCUT) - 1):
+        a, b = 4 * XCUT[i], 4 * XCUT[i + 1]
+        sy.dma_start(T.xt[:, a:b], T.x[:, a:b]).then_inc(S["x%d" % i], 16)
     for k in range(2):
         for q in range(4):
             r = 16 * k + 4 * q
@@ -80,7 +92,7 @@ def rank_program(g, core, T, topo):
         sy.dma_start(T.s2[16 * k:16 * k + 16, :], T.so[:]).then_inc(S.s2l, 16)
 
     plan = receivers(core, T.cores, topo)
-    pal = [dst for dst, _, _ in plan if topo.die(dst) == topo.die(core)][0]
+    pal = [dst for dst in plan if topo.die(dst) == topo.die(core)][0]
     low = rank < T.rank_of(pal)
     first = (0, 128) if low else (TOK - 128, TOK)
     give = (0, PART) if low else (TOK - PART, TOK)
@@ -99,13 +111,20 @@ def rank_program(g, core, T, topo):
         a, b = lo // 4, hi // 4
         g.affine_select(T.ident[:, a:b], T.ones[:, a:b], [[-1, b - a]], AluOpType.is_equal, 0.0, -a, 1).then_inc(sem, 1)
 
-    def ones_of(cols, sem):
+    def ones_of(q, cols, sem):
         for t in range(4):
-            v.tensor_copy(T.et[:, 4 * cols[0] + 5 * t:4 * cols[1]:16], T.ident[:, cols[0] // 4:cols[1] // 4]).then_inc(sem, 1)
+            out, src = T.et[:, 4 * cols[0] + 5 * t:4 * cols[1]:16], T.ident[:, cols[0] // 4:cols[1] // 4]
+            (v.tensor_copy(out, src) if q is v else sc.activation(out, src, Copy)).then_inc(sem, 1)
+
+    def ones_rest(q):
+        q.wait_ge(S.gidb, 1)
+        q.wait_ge(S.vezb, 1)
+        q.wait_ge(S.sez, len(parts))
+        ones_of(q, rest, S.veb)
 
     v.wait_ge(S.vez, 1)
     v.wait_ge(S.gida, 1)
-    ones_of(first, S.vea)
+    ones_of(v, first, S.vea)
     v.wait_ge(S.vea, 4)
     v.quantize_mx(T.eq[:, first[0]:first[1]], T.es[:, first[0]:first[1]],
                   T.et[:, 4 * first[0]:4 * first[1]]).then_inc(S.veqa, 1)
@@ -120,14 +139,14 @@ def rank_program(g, core, T, topo):
     v.wait_ge(S.snl, 32)
     for k in range(4):
         v.tensor_copy(T.lst[32 * k:32 * k + 32, :], T.sn2[:]).then_inc(S.vlst, 1)
-    v.wait_ge(S.x0, 16)
-    v.quantize_mx(T.xq[:, 0:XA], T.xs[:, 0:XA], T.xt[:, 0:4 * XA]).then_inc(S.qx, 1)
-    v.wait_ge(S.x1, 16)
-    v.quantize_mx(T.xq[:, XA:TOK], T.xs[:, XA:TOK], T.xt[:, 4 * XA:4 * TOK]).then_inc(S.qx, 1)
+    for i in range(len(XCUT) - 1):
+        a, b = XCUT[i], XCUT[i + 1]
+        v.wait_ge(S["x%d" % i], 16)
+        v.quantize_mx(T.xq[:, a:b], T.xs[:, a:b], T.xt[:, 4 * a:4 * b]).then_inc(S.qx, 1)
 
     for q in (v, sc):
         q.wait_ge(S.vlst, 4)
-        q.wait_ge(S.qx, 2)
+        q.wait_ge(S.qx, len(XCUT) - 1)
 
     def pick(d, code, scale, c_sem, s_sem):
         lo, hi = CAPP * d, CAPP * (d + 1)
@@ -136,91 +155,108 @@ def rank_program(g, core, T, topo):
         sc.activation(scale[:, lo:hi], T.xs[:, 0:TOK].indirect(off), Copy).then_inc(s_sem, 1)
 
     own = slice(CAPP * rank, CAPP * (rank + 1))
-    codes, scales = [], []
-    for i, (dst, ec, es) in enumerate(plan):
-        d = T.rank_of(dst)
-        pick(d, T.slotq, T.slots, S["pc%d" % i], S["ps%d" % i])
-        rid, pid, _ = topo.addr(dst)
-        cut = slice(CAPP * d, CAPP * (d + 1))
-        codes.append(RemoteDMATransfer(dst_ids=[DstId(rid=rid, pnc=pid)], dma_engine_mask=bits(ec), remote_sem=S.arrc,
-                                       src=T.slotq[:, cut].bitcast(u8), dst=T.landq[:, own].bitcast(u8)))
-        scales.append(RemoteDMATransfer(dst_ids=[DstId(rid=rid, pnc=pid)], dma_engine_mask=bits(es), remote_sem=S.arrs,
-                                        src=T.slots[:, cut], dst=T.lands[:, own]))
+    for i, dst in enumerate(plan):
+        pick(T.rank_of(dst), T.slotq, T.slots, S["kc%d" % i], S["ks%d" % i])
     pick(rank, T.landq, T.lands, S.ownc, S.owns)
-    g.wait_ge(S.pc0, 1)
-    g.remote_dma_fused(codes[:1], local_sem=S.snd)
-    g.wait_ge(S.pc1, 1)
-    g.wait_ge(S.pc2, 1)
-    g.remote_dma_fused(codes[1:], local_sem=S.snd)
-    for i in range(3):
-        g.wait_ge(S["ps%d" % i], 1)
-    g.remote_dma_fused(scales, local_sem=S.snd)
-    g.wait_ge(S.snd, 2 * len(every) + sum(len(ec) + len(es) for _, ec, es in plan))
-    arrive = [e for src in T.cores for e in receivers(src, T.cores, topo) if e[0] == core]
+    sent = 2 * len(every)
+    for call in sends(core, T.cores, topo):
+        transfers = []
+        for kind, i, dst, engines in call:
+            g.wait_ge(S["k" + kind + str(i)], 1)
+            rid, pid, _ = topo.addr(dst)
+            d = T.rank_of(dst)
+            cut = slice(CAPP * d, CAPP * (d + 1))
+            src, to, sem = ((T.slotq[:, cut].bitcast(u8), T.landq[:, own].bitcast(u8), S.arrc) if kind == "c" else
+                            (T.slots[:, cut], T.lands[:, own], S.arrs))
+            transfers.append(RemoteDMATransfer(dst_ids=[DstId(rid=rid, pnc=pid)], dma_engine_mask=bits(engines),
+                                               remote_sem=sem, src=src, dst=to))
+            sent += len(engines)
+        g.remote_dma_fused(transfers, local_sem=S.snd)
+    g.wait_ge(S.snd, sent)
+    arrive = {kind: sum(len(e[3]) for src in T.cores for call in sends(src, T.cores, topo) for e in call
+                        if e[2] == core and e[0] == kind) for kind in "cs"}
 
-    v.wait_ge(S.gidb, 1)
-    v.wait_ge(S.vezb, 1)
-    v.wait_ge(S.sez, len(parts))
-    ones_of(rest, S.veb)
+    ones_rest(sc)
     v.wait_ge(S.m2l, 16 * 8)
     for k in range(4):
         v.tensor_copy(T.lp[32 * k:32 * k + 32, :], T.m2[:, :, 0:32:4]).then_inc(S.vlp, 1)
-    v.wait_ge(S.veb, 4)
-    v.quantize_mx(T.eq[:, rest[0]:rest[1]], T.es[:, rest[0]:rest[1]], T.et[:, z0:z1]).then_inc(S.veqb, 1)
     v.wait_ge(S.s2l, 16 * 4)
     for k in range(2):
         v.tensor_copy(T.ln[64 * k:64 * k + 64, :], T.s2[:]).then_inc(S.vln, 1)
+    v.wait_ge(S.veb, 4)
+    v.quantize_mx(T.eq[:, rest[0]:rest[1]], T.es[:, rest[0]:rest[1]], T.et[:, z0:z1]).then_inc(S.veqb, 1)
 
-    te.wait_ge(S.veqa, 1)
-    te.wait_ge(S.veqb, 1)
-    te.wait_ge(S.arre, 2 * len(topo.engines(pal, core)))
-    for t in range(4):
-        te.wait_ge(S["fc%d" % (t // 2)], 1)
-        te.wait_ge(S["fs%d" % (t // 2)], 1)
-        te.matmul_mx(T.pp[:, 512 * t:512 * t + 512], T.fpq[:, 128 * t:128 * t + 128], T.fps[:, 128 * t:128 * t + 128],
-                     T.eq[:, 0:512], T.es[:, 0:512], True, True).then_inc(S["mm%d" % t], 1)
+    items = VQ + SQ
+    seen = set()
 
-    v.wait_ge(S.vlp, 4)
-    v.wait_ge(S.ownc, 1)
-    v.wait_ge(S.arrc, sum(len(ec) for _, ec, _ in arrive))
-    for h in range(2):
-        v.tensor_copy(T.fpq[:, 256 * h:256 * h + 256].bitcast(u32),
-                      T.landq[:, 0:512].bitcast(u32).indirect(T.lp[:, 16 * h:16 * h + 16])).then_inc(S["fc%d" % h], 1)
-    v.wait_ge(S.vln, 2)
-    v.tensor_copy(T.fnq[:, 0:512].bitcast(u32),
-                  T.landq[:, 0:512].bitcast(u32).indirect(T.ln[:, 0:32])).then_inc(S.fnc, 1)
-    for t in COPY_V:
-        v.wait_ge(S["mm%d" % t], 1)
-        v.tensor_copy(T.bt[:, t:2048:4], T.pp[:, 512 * t:512 * t + 512]).then_inc(S.cv, 1)
-    v.wait_ge(S.cs, len(COPY_S))
-    v.wait_ge(S.cv, len(COPY_V))
-    for h, (lo, hi) in enumerate(RUNS):
-        v.quantize_mx(T.btq[:, lo:hi], T.bts[:, lo:hi], T.bt[:, 4 * lo:4 * hi]).then_inc(S["q%d" % h], 1)
+    def need(q, sem, n=1):
+        if (q[0], sem) not in seen:
+            seen.add((q[0], sem))
+            q[1].wait_ge(S[sem], n)
 
-    sc.wait_ge(S.vlp, 4)
-    sc.wait_ge(S.owns, 1)
-    sc.wait_ge(S.arrs, sum(len(es) for _, _, es in arrive))
-    for h in range(2):
-        sc.activation(T.fps[:, 256 * h:256 * h + 256],
-                      T.lands[:, 0:512].indirect(T.lp[:, 16 * h:16 * h + 16]), Copy).then_inc(S["fs%d" % h], 1)
-    for t in COPY_S:
-        sc.wait_ge(S["mm%d" % t], 1)
-        sc.activation(T.bt[:, t:2048:4], T.pp[:, 512 * t:512 * t + 512], Copy).then_inc(S.cs, 1)
-    sc.wait_ge(S.vln, 2)
-    sc.activation(T.fns[:, 0:512], T.lands[:, 0:512].indirect(T.ln[:, 0:32]), Copy).then_inc(S.fnsc, 1)
+    def covers(q, kind, lo, hi):
+        for it in items:
+            if it[0] == kind and it[1] < hi and it[2] > lo:
+                need(q, name(it))
 
-    sy.wait_ge(S.fnc, 1)
-    sy.dma_start(T.fc[:, 0:2048], T.fnq[:, 0:512].bitcast(u8)).then_inc(S.stsy, 16)
-    for h, (lo, hi) in enumerate(RUNS):
-        sy.wait_ge(S["q%d" % h], 1)
-        sy.dma_start(T.bc[:, 4 * lo:4 * hi], T.btq[:, lo:hi].bitcast(u8)).then_inc(S.stsy, 16)
-    for k in range(3):
-        sy.dma_start(T.bs[4 * k:4 * k + 4, 0:512], T.bts[32 * k:32 * k + 4, 0:512]).then_inc(S.stsy, 16)
-    sc.wait_ge(S.fnsc, 1)
-    for k in range(4):
-        sc.dma_start(T.fs[4 * k:4 * k + 4, 0:512], T.fns[32 * k:32 * k + 4, 0:512]).then_inc(S.stsc, 16)
-    sc.wait_ge(S.q0, 1)
-    sc.wait_ge(S.q1, 1)
-    sc.dma_start(T.bs[12:16, 0:512], T.bts[96:100, 0:512]).then_inc(S.stsc, 16)
-    sy.wait_ge(S.stsy, 16 * 6)
-    sc.wait_ge(S.stsc, 16 * 5)
+    pe = ("t", te)
+    need(pe, "veqa")
+    need(pe, "veqb")
+    need(pe, "arre", 2 * len(topo.engines(pal, core)))
+    for i, (t, lo, hi) in enumerate(MM):
+        cols = slice(128 * t, 128 * t + 128)
+        covers(pe, "pc", cols.start, cols.stop)
+        covers(pe, "ps", cols.start, cols.stop)
+        te.matmul_mx(T.pp[:, 512 * i:512 * i + hi - lo], T.fpq[:, cols], T.fps[:, cols],
+                     T.eq[:, lo:hi], T.es[:, lo:hi], True, True).then_inc(S["mm%d" % i], 1)
+
+    def run(q, order, stored):
+        on_v, stores = q[0] == "v", 0
+
+        def copy(to, src):
+            return v.tensor_copy(to, src) if on_v else sc.activation(to, src, Copy)
+
+        for it in order:
+            kind = it[0]
+            if kind in ("pc", "nc", "ps", "ns"):
+                lo, hi = it[1:]
+                by_place = kind[0] == "n"
+                need(q, *(("vln", 2) if by_place else ("vlp", 4)))
+                need(q, "own" + kind[1])
+                need(q, "arr" + kind[1], arrive[kind[1]])
+                off = (T.ln if by_place else T.lp)[:, lo // 16:hi // 16]
+                if kind[1] == "c":
+                    call = copy((T.fnq if by_place else T.fpq)[:, lo:hi].bitcast(u32),
+                                T.landq[:, 0:TOK].bitcast(u32).indirect(off))
+                else:
+                    call = copy((T.fns if by_place else T.fps)[:, lo:hi], T.lands[:, 0:TOK].indirect(off))
+                call.then_inc(S[name(it)], 1)
+            elif kind == "cp":
+                i = it[1]
+                t, lo, hi = MM[i]
+                need(q, "mm%d" % i)
+                copy(T.bt[:, 4 * lo + t:4 * hi:4], T.pp[:, 512 * i:512 * i + hi - lo]).then_inc(S[name(it)], 1)
+            elif kind == "q":
+                lo, hi = it[1:]
+                for i, m in enumerate(MM):
+                    if m[1] < hi and m[2] > lo:
+                        need(q, "cp%d" % i)
+                v.quantize_mx(T.btq[:, lo:hi], T.bts[:, lo:hi], T.bt[:, 4 * lo:4 * hi]).then_inc(S[name(it)], 1)
+            elif kind in ("fc", "bc"):
+                lo, hi = it[1:]
+                covers(q, "nc" if kind == "fc" else "q", lo, hi)
+                src = T.fnq if kind == "fc" else T.btq
+                q[1].dma_start(T[kind][:, 4 * lo:4 * hi], src[:, lo:hi].bitcast(u8)).then_inc(S[stored], 16)
+                stores += 1
+            else:
+                k = it[1]
+                covers(q, "ns" if kind == "fs" else "q", 0, TOK)
+                src = T.fns if kind == "fs" else T.bts
+                q[1].dma_start(T[kind][4 * k:4 * k + 4, 0:TOK], src[32 * k:32 * k + 4, 0:TOK]).then_inc(S[stored], 16)
+                stores += 1
+        if stores:
+            q[1].wait_ge(S[stored], 16 * stores)
+
+    run(("v", v), VQ, None)
+    run(("s", sc), SQ, "stsc")
+    run(("y", sy), YQ, "stsy")

from concourse.bass import DstId, RemoteDMATransfer
from concourse.mybir import dt, AluOpType, ActivationFunctionType

N = 4
CAPP = 128
TOK = 512
XCUT = (0, 336, 512)
PART = 32
ZV = 480
ONES = "sl"
SENDS = (("c0",), ("s0",), ("c1",), ("s1",), ("c2",), ("s2",))
RECV = "ffn"
MM = [(t, 0, 512) for t in range(4)]
VQ = [("pc", 0, 256), ("pc", 256, 512), ("nc", 0, 512), ("cp", 2), ("cp", 3), ("q", 0, 256), ("q", 256, 512)]
SQ = [("ps", 0, 256), ("ps", 256, 512), ("cp", 0), ("cp", 1), ("ns", 0, 512), ("fs", 0), ("fs", 1), ("fs", 2), ("fs", 3), ("bs", 3)]
YQ = [("fc", 0, 512), ("bc", 0, 256), ("bc", 256, 512), ("bs", 0), ("bs", 1), ("bs", 2)]

SCRATCH = {
    "xt": ("sbuf", [128, 4 * TOK], "bfloat16"),
    "sn2": ("sbuf", [32, 32], "int32"),
    "lst": ("sbuf", [128, 32], "uint16"),
    "m2": ("sbuf", [32, 4, 32], "int32"),
    "lp": ("sbuf", [128, 32], "uint16"),
    "s2": ("sbuf", [64, 32], "int32"),
    "ln": ("sbuf", [128, 32], "uint16"),
    "ones": ("sbuf", [128, 128], "bfloat16"),
    "ident": ("sbuf", [128, 128], "bfloat16"),
    "et": ("sbuf", [128, 2048], "bfloat16"),
    "pp": ("psum", [128, 4096], "float32"),
    "bt": ("sbuf", [128, 2048], "bfloat16"),
}
for _n, _w in (("x", 512), ("slot", 512), ("land", 512), ("e", 512), ("fp", 512), ("fn", 512), ("bt", 512)):
    SCRATCH[_n + "q"] = ("sbuf", [128, _w], "float8_e4m3fn_x4")
    SCRATCH[_n + "s"] = ("sbuf", [128, _w], "uint8")


def name(item):
    return item[0] + str(item[1])


SEMAPHORES = (
    ["snl", "m2l", "s2l", "stsy", "stsc", "vones", "vez", "vea", "vezb", "sez", "gida", "gidb", "veb",
     "veqa", "veqb", "arre", "qx", "vlst", "ownc", "owns", "vln", "vlp", "snd", "arrc", "arrs"]
    + ["x%d" % i for i in range(len(XCUT) - 1)]
    + ["kc%d" % i for i in range(3)] + ["ks%d" % i for i in range(3)]
    + ["mm%d" % t for t in range(len(MM))]
    + [name(i) for i in VQ + SQ if i[0] not in ("fs", "bs", "fc", "bc")])


def receivers(src, cores, topo):
    mine = [c for c in cores if topo.die(c) == topo.die(src)]
    far = [c for c in cores if topo.die(c) != topo.die(src)]
    k = mine.index(src)
    far = far[k:] + far[:k]
    near = [c for c in mine if c != src]
    pool = {"f": far, "n": near}
    return [pool[w].pop(0) for w in RECV]


def sends(src, cores, topo):
    plan = receivers(src, cores, topo)
    return [[(w[0], int(w[1]), plan[int(w[1])], topo.engines(src, plan[int(w[1])])[k::len(call)])
             for k, w in enumerate(call)] for call in SENDS]


def bits(engines):
    m = 0
    for e in engines:
        m |= 1 << e
    return m


def rank_program(g, core, T, topo):
    rank = T.rank_of(core)
    if rank is None:
        return
    S = T.sem
    v, sc, te, sy = g.vector, g.scalar, g.tensor, g.sync
    Copy = ActivationFunctionType.Copy
    u32, u8 = dt.uint32, dt.uint8

    for k, q in enumerate((sy, sc)):
        q.dma_start(T.sn2[16 * k:16 * k + 16, :], T.sn[:]).then_inc(S.snl, 16)
    for i in range(len(XCUT) - 1):
        a, b = 4 * XCUT[i], 4 * XCUT[i + 1]
        sy.dma_start(T.xt[:, a:b], T.x[:, a:b]).then_inc(S["x%d" % i], 16)
    for k in range(2):
        for q in range(4):
            r = 16 * k + 4 * q
            sy.dma_start(T.m2[r:r + 4, :, 0:32 - q], T.so[:, q:32]).then_inc(S.m2l, 16)
    for k in range(4):
        sy.dma_start(T.s2[16 * k:16 * k + 16, :], T.so[:]).then_inc(S.s2l, 16)

    plan = receivers(core, T.cores, topo)
    pal = [dst for dst in plan if topo.die(dst) == topo.die(core)][0]
    low = rank < T.rank_of(pal)
    first = (0, 128) if low else (TOK - 128, TOK)
    give = (0, PART) if low else (TOK - PART, TOK)
    rest = (128, TOK - PART) if low else (PART, TOK - 128)
    z0, z1 = 4 * rest[0], 4 * rest[1]
    v.memset(T.ones[:], 1.0).then_inc(S.vones, 1)
    v.memset(T.et[:, 4 * first[0]:4 * first[1]], 0.0).then_inc(S.vez, 1)
    v.memset(T.et[:, z0:z0 + ZV], 0.0).then_inc(S.vezb, 1)
    sc.wait_ge(S.vezb, 1)
    parts = range(z0 + ZV, z1, ZV)
    for a in parts:
        w = min(ZV, z1 - a)
        sc.activation(T.et[:, a:a + w], T.et[:, z0:z0 + w], Copy).then_inc(S.sez, 1)
    g.wait_ge(S.vones, 1)
    for (lo, hi), sem in ((first, S.gida), (rest, S.gidb)):
        a, b = lo // 4, hi // 4
        g.affine_select(T.ident[:, a:b], T.ones[:, a:b], [[-1, b - a]], AluOpType.is_equal, 0.0, -a, 1).then_inc(sem, 1)

    def ones_of(q, cols, sem):
        for t in range(4):
            out, src = T.et[:, 4 * cols[0] + 5 * t:4 * cols[1]:16], T.ident[:, cols[0] // 4:cols[1] // 4]
            (v.tensor_copy(out, src) if q is v else sc.activation(out, src, Copy)).then_inc(sem, 1)

    def ones_rest(q):
        q.wait_ge(S.gidb, 1)
        q.wait_ge(S.vezb, 1)
        q.wait_ge(S.sez, len(parts))
        ones_of(q, rest, S.veb)

    v.wait_ge(S.vez, 1)
    v.wait_ge(S.gida, 1)
    ones_of(v, first, S.vea)
    v.wait_ge(S.vea, 4)
    v.quantize_mx(T.eq[:, first[0]:first[1]], T.es[:, first[0]:first[1]],
                  T.et[:, 4 * first[0]:4 * first[1]]).then_inc(S.veqa, 1)
    rid, pid, _ = topo.addr(pal)
    every = topo.engines(core, pal)
    cut = slice(*give)
    g.wait_ge(S.veqa, 1)
    for part in (T.eq[:, cut].bitcast(u8), T.es[:, cut]):
        g.remote_dma_fused([RemoteDMATransfer(dst_ids=[DstId(rid=rid, pnc=pid)], dma_engine_mask=bits(every),
                                              remote_sem=S.arre, src=part, dst=part)], local_sem=S.snd)

    v.wait_ge(S.snl, 32)
    for k in range(4):
        v.tensor_copy(T.lst[32 * k:32 * k + 32, :], T.sn2[:]).then_inc(S.vlst, 1)
    for i in range(len(XCUT) - 1):
        a, b = XCUT[i], XCUT[i + 1]
        v.wait_ge(S["x%d" % i], 16)
        v.quantize_mx(T.xq[:, a:b], T.xs[:, a:b], T.xt[:, 4 * a:4 * b]).then_inc(S.qx, 1)

    for q in (v, sc):
        q.wait_ge(S.vlst, 4)
        q.wait_ge(S.qx, len(XCUT) - 1)

    def pick(d, code, scale, c_sem, s_sem):
        lo, hi = CAPP * d, CAPP * (d + 1)
        off = T.lst[:, 8 * d:8 * d + 8]
        v.tensor_copy(code[:, lo:hi].bitcast(u32), T.xq[:, 0:TOK].bitcast(u32).indirect(off)).then_inc(c_sem, 1)
        sc.activation(scale[:, lo:hi], T.xs[:, 0:TOK].indirect(off), Copy).then_inc(s_sem, 1)

    own = slice(CAPP * rank, CAPP * (rank + 1))
    for i, dst in enumerate(plan):
        pick(T.rank_of(dst), T.slotq, T.slots, S["kc%d" % i], S["ks%d" % i])
    pick(rank, T.landq, T.lands, S.ownc, S.owns)
    sent = 2 * len(every)
    for call in sends(core, T.cores, topo):
        transfers = []
        for kind, i, dst, engines in call:
            g.wait_ge(S["k" + kind + str(i)], 1)
            rid, pid, _ = topo.addr(dst)
            d = T.rank_of(dst)
            cut = slice(CAPP * d, CAPP * (d + 1))
            src, to, sem = ((T.slotq[:, cut].bitcast(u8), T.landq[:, own].bitcast(u8), S.arrc) if kind == "c" else
                            (T.slots[:, cut], T.lands[:, own], S.arrs))
            transfers.append(RemoteDMATransfer(dst_ids=[DstId(rid=rid, pnc=pid)], dma_engine_mask=bits(engines),
                                               remote_sem=sem, src=src, dst=to))
            sent += len(engines)
        g.remote_dma_fused(transfers, local_sem=S.snd)
    g.wait_ge(S.snd, sent)
    arrive = {kind: sum(len(e[3]) for src in T.cores for call in sends(src, T.cores, topo) for e in call
                        if e[2] == core and e[0] == kind) for kind in "cs"}

    ones_rest(sc)
    v.wait_ge(S.m2l, 16 * 8)
    for k in range(4):
        v.tensor_copy(T.lp[32 * k:32 * k + 32, :], T.m2[:, :, 0:32:4]).then_inc(S.vlp, 1)
    v.wait_ge(S.s2l, 16 * 4)
    for k in range(2):
        v.tensor_copy(T.ln[64 * k:64 * k + 64, :], T.s2[:]).then_inc(S.vln, 1)
    v.wait_ge(S.veb, 4)
    v.quantize_mx(T.eq[:, rest[0]:rest[1]], T.es[:, rest[0]:rest[1]], T.et[:, z0:z1]).then_inc(S.veqb, 1)

    items = VQ + SQ
    seen = set()

    def need(q, sem, n=1):
        if (q[0], sem) not in seen:
            seen.add((q[0], sem))
            q[1].wait_ge(S[sem], n)

    def covers(q, kind, lo, hi):
        for it in items:
            if it[0] == kind and it[1] < hi and it[2] > lo:
                need(q, name(it))

    pe = ("t", te)
    need(pe, "veqa")
    need(pe, "veqb")
    need(pe, "arre", 2 * len(topo.engines(pal, core)))
    for i, (t, lo, hi) in enumerate(MM):
        cols = slice(128 * t, 128 * t + 128)
        covers(pe, "pc", cols.start, cols.stop)
        covers(pe, "ps", cols.start, cols.stop)
        te.matmul_mx(T.pp[:, 512 * i:512 * i + hi - lo], T.fpq[:, cols], T.fps[:, cols],
                     T.eq[:, lo:hi], T.es[:, lo:hi], True, True).then_inc(S["mm%d" % i], 1)

    def run(q, order, stored):
        on_v, stores = q[0] == "v", 0

        def copy(to, src):
            return v.tensor_copy(to, src) if on_v else sc.activation(to, src, Copy)

        for it in order:
            kind = it[0]
            if kind in ("pc", "nc", "ps", "ns"):
                lo, hi = it[1:]
                by_place = kind[0] == "n"
                need(q, *(("vln", 2) if by_place else ("vlp", 4)))
                need(q, "own" + kind[1])
                need(q, "arr" + kind[1], arrive[kind[1]])
                off = (T.ln if by_place else T.lp)[:, lo // 16:hi // 16]
                if kind[1] == "c":
                    call = copy((T.fnq if by_place else T.fpq)[:, lo:hi].bitcast(u32),
                                T.landq[:, 0:TOK].bitcast(u32).indirect(off))
                else:
                    call = copy((T.fns if by_place else T.fps)[:, lo:hi], T.lands[:, 0:TOK].indirect(off))
                call.then_inc(S[name(it)], 1)
            elif kind == "cp":
                i = it[1]
                t, lo, hi = MM[i]
                need(q, "mm%d" % i)
                copy(T.bt[:, 4 * lo + t:4 * hi:4], T.pp[:, 512 * i:512 * i + hi - lo]).then_inc(S[name(it)], 1)
            elif kind == "q":
                lo, hi = it[1:]
                for i, m in enumerate(MM):
                    if m[1] < hi and m[2] > lo:
                        need(q, "cp%d" % i)
                v.quantize_mx(T.btq[:, lo:hi], T.bts[:, lo:hi], T.bt[:, 4 * lo:4 * hi]).then_inc(S[name(it)], 1)
            elif kind in ("fc", "bc"):
                lo, hi = it[1:]
                covers(q, "nc" if kind == "fc" else "q", lo, hi)
                src = T.fnq if kind == "fc" else T.btq
                q[1].dma_start(T[kind][:, 4 * lo:4 * hi], src[:, lo:hi].bitcast(u8)).then_inc(S[stored], 16)
                stores += 1
            else:
                k = it[1]
                covers(q, "ns" if kind == "fs" else "q", 0, TOK)
                src = T.fns if kind == "fs" else T.bts
                q[1].dma_start(T[kind][4 * k:4 * k + 4, 0:TOK], src[32 * k:32 * k + 4, 0:TOK]).then_inc(S[stored], 16)
                stores += 1
        if stores:
            q[1].wait_ge(S[stored], 16 * stores)

    run(("v", v), VQ, None)
    run(("s", sc), SQ, "stsc")
    run(("y", sy), YQ, "stsy")
